import numpy as np
import ml_dtypes


def mxq(x, axis, fmt="e4m3"):
    dtype, down = {"e4m3": (ml_dtypes.float8_e4m3fn, 7), "e5m2": (ml_dtypes.float8_e5m2, 14)}[fmt]
    v = np.moveaxis(np.asarray(x, np.float32).astype(ml_dtypes.bfloat16).astype(np.float64), axis, -1)
    blocks = v.reshape(v.shape[:-1] + (-1, 32))
    amax = np.abs(blocks).max(-1, keepdims=True)
    byte = np.maximum(np.where(amax > 0, np.frexp(amax)[1] - 1 + 127, 0) - down, 1)
    scale = np.exp2(byte - 127.0)
    codes = (blocks / scale).astype(np.float32).astype(dtype).astype(np.float64)
    return np.moveaxis((codes * scale).reshape(v.shape), -1, axis)


WIDE = False


def mx_kscale(k):
    if not WIDE:
        return np.ones(k)
    levels = np.array([10, -10, 5, -5, 0])
    if k % 512:
        return np.exp2(np.random.permutation(np.resize(levels, k // 32))).repeat(32)
    a = np.empty((k // 512, 16))
    for p in range(k // 512):
        a[p, :8] = np.random.permutation(np.resize(levels, 8))
        for g in range(8):
            far = levels[np.abs(levels - a[p, g]) >= 10]
            a[p, g + 8] = far[np.random.randint(len(far))]
    return np.exp2(a.ravel()).repeat(32)


def f64(x):
    return np.asarray(x).astype(np.float64)


def striped8(idx):
    return np.asarray(idx).reshape(8, -1, 16).transpose(0, 2, 1).reshape(128, -1).astype(np.uint16)


def unstriped8(offs):
    return offs.reshape(8, 16, -1).transpose(0, 2, 1).reshape(8, -1).astype(np.int64)


def pick8(x, idx, run):
    r = np.arange(len(x))
    return x[r[:, None], idx[r % (8 * run) // run]]


E2M1 = np.array([0.0, 0.5, 1.0, 1.5, 2.0, 3.0, 4.0, 6.0, -0.0, -0.5, -1.0, -1.5, -2.0, -3.0, -4.0, -6.0])


def pack_weight(w, fmt):
    k, n = w.shape
    w = f64(np.asarray(w, np.float32).astype(ml_dtypes.bfloat16)).reshape(k // 32, 32, n)
    amax = np.abs(w).max(1)
    if fmt == "e4m3":
        byte = np.frexp(amax)[1] - 1 + 127 - 7
    else:
        mant, ex = np.frexp(amax / 6.0)
        byte = np.where(mant > 0.5, ex, ex - 1) + 127
    byte = np.clip(np.where(amax > 0, byte, 1), 1, 254)
    scaled = (w * np.exp2(127.0 - byte)[:, None, :]).reshape(k, n).astype(np.float32)
    by_word = np.ascontiguousarray(scaled.reshape(k // 512, 128, 4, n).transpose(0, 1, 3, 2))
    if fmt == "e4m3":
        words = by_word.astype(ml_dtypes.float8_e4m3fn).view(np.uint8)
    else:
        c = by_word.astype(ml_dtypes.float4_e2m1fn).view(np.uint8) & 0xF
        words = (c[..., 0::2] | (c[..., 1::2] << 4)).reshape(k // 512, 128, 2 * n)
    return np.ascontiguousarray(words), np.ascontiguousarray(byte.astype(np.uint8).reshape(k // 512, 16, n))


def unpack_weight(words, scales, fmt):
    g, _, n = scales.shape
    words = np.ascontiguousarray(words).reshape(g, 128, n, -1)
    if fmt == "e4m3":
        vals = words.view(ml_dtypes.float8_e4m3fn).astype(np.float64)
    else:
        nib = np.empty((g, 128, n, 4), np.uint8)
        nib[..., 0::2] = words & 0xF
        nib[..., 1::2] = words >> 4
        vals = E2M1[nib]
    vals = vals * np.repeat(np.exp2(scales.astype(np.float64) - 127.0), 8, axis=1)[..., None]
    return vals.transpose(0, 1, 3, 2).reshape(g * 512, n)


K, T, J, N = 1024, 1024, 512, 512


def setup_inputs():
    n = np.random.standard_normal
    idx = np.stack([np.random.permutation(T)[:J] for _ in range(8)])
    idx2 = np.stack([np.random.permutation(T)[:J] for _ in range(8)])
    fk = mx_kscale(K)
    wp = pack_weight(n((K, N)) * 1 / np.sqrt(K) * fk[:, None], "e2m1")
    return {
        "xf": (n((K, T))).astype(np.float32),
        "fk": (np.random.uniform(0.5, 2.0, (K, 1)) / fk[:, None]).astype(np.float32),
        "w_words": wp[0],
        "w_scales": wp[1],
        "rw": (np.random.uniform(0.5, 2.0, (1, J))).astype(np.float32),
        "offs": striped8(idx),
        "offs2": striped8(idx2),
    }


def reference(xf, fk, w_words, w_scales, rw, offs, offs2):
    idx = unstriped8(offs)
    idx2 = unstriped8(offs2)
    wu = unpack_weight(w_words, w_scales, "e2m1")
    u = np.maximum(pick8(f64(xf), idx, 64), pick8(f64(xf), idx2, 64)) * f64(fk)
    uq = mxq(u, 0, "e4m3")
    p = wu.T @ uq
    y = p * f64(rw)
    return y

@@ -1,0 +1,161 @@
+from contextlib import ExitStack
+
+import concourse.mybir as mybir
+
+K, T, J, N = 1024, 1024, 512, 512
+FLOPS = 2 * K * N * J
+
+F32 = mybir.dt.float32
+BF16 = mybir.dt.bfloat16
+I32 = mybir.dt.int32
+U32 = mybir.dt.uint32
+U16 = mybir.dt.uint16
+U8 = mybir.dt.uint8
+FP8X4 = mybir.dt.float8_e4m3fn_x4
+FP4X4 = mybir.dt.float4_e2m1fn_x4
+MAX = mybir.AluOpType.max
+MULT = mybir.AluOpType.mult
+COPY = mybir.ActivationFunctionType.Copy
+
+P = 128
+PACK = 4
+PASSES = K // (P * PACK)
+BLK = 128
+NT = N // P
+JB = J // BLK
+
+
+def tile_list_head_larger_inputs_kernel(tc, xf, fk, w_words, w_scales, rw, offs, offs2, out):
+    nc = tc.nc
+    with ExitStack() as ctx:
+        lists = ctx.enter_context(tc.tile_pool(name="lists", bufs=1))
+        keep = ctx.enter_context(tc.tile_pool(name="keep", bufs=1))
+        psum = ctx.enter_context(tc.psum_pool(name="psum", bufs=1))
+
+        list_a = lists.tile([P, J // 16], U16, name="list_a")
+        list_b = lists.tile([P, J // 16], U16, name="list_b")
+        x_rows = xf.rearrange("(a p t) c -> a t p c", a=PASSES, t=PACK)
+        x = [[keep.tile([P, T], F32, name=f"x{a}{t}") for t in range(PACK)] for a in range(PASSES)]
+        factor = keep.tile([P, PASSES, PACK], F32, name="factor")
+        w_codes = keep.tile([P, PASSES, 2 * N], U8, name="w_codes", align_bytes=64)
+        w_plane = keep.tile([P, PASSES, N], U8, name="w_plane", align_bytes=64)
+        slot_w = keep.tile([P, J], F32, name="slot_w")
+
+        nc.gpsimd.memset(w_plane[:].rearrange("p a n -> p (a n)").bitcast(I32), 0)
+        nc.sync.dma_start(list_a[:], offs)
+        nc.sync.dma_start(x[0][0][:], x_rows[0, 0])
+        nc.sync.dma_start(list_b[:], offs2)
+        nc.sync.dma_start(x[0][1][:], x_rows[0, 1])
+        nc.sync.dma_start(factor[:], fk.rearrange("(a p t) o -> p a (t o)", a=PASSES, t=PACK))
+        nc.sync.dma_start(x[0][2][:], x_rows[0, 2])
+        nc.sync.dma_start(x[0][3][:], x_rows[0, 3])
+        for t in range(PACK):
+            nc.sync.dma_start(x[1][t][:], x_rows[1, t])
+        nc.sync.dma_start(w_codes[:].bitcast(I32), w_words.rearrange("a p n -> p a n").bitcast(I32))
+        for q in range(4):
+            nc.sync.dma_start(
+                w_plane[32 * q : 32 * q + 4].bitcast(I32),
+                w_scales[:, 4 * q : 4 * q + 4, :].rearrange("a r n -> r a n").bitcast(I32),
+            )
+        nc.sync.dma_start(slot_w[:], rw[0].partition_broadcast(P))
+
+        banks = [psum.tile([P, NT, BLK], F32, name=f"bank{b}") for b in range(JB)]
+        out_rows = out.rearrange("(c p) j -> p c j", p=P)
+
+        def pick(a, t, offsets, j0, width, name):
+            picked = keep.tile([P, width], F32, name=name)
+            nc.vector.tensor_copy(picked[:], x[a][t][:].indirect(offsets[:, j0 // 16 : (j0 + width) // 16]))
+            return picked
+
+        def larger(pa, pb, c0, width, name):
+            m = keep.tile([P, width], F32, name=name)
+            nc.vector.tensor_tensor(m[:], pa[:, c0 : c0 + width], pb[:, c0 : c0 + width], MAX)
+            return m
+
+        def scale(grouped, m, c0, width, a, t):
+            nc.scalar.activation(grouped[:, :, t], m[:, c0 : c0 + width], COPY, scale=factor[:, a, t : t + 1])
+
+        def quantise(grouped, width, name):
+            codes = keep.tile([P, width], U32, name=name + "c", align_bytes=64)
+            plane = keep.tile([P, width], U8, name=name + "s", align_bytes=64)
+            nc.vector.quantize_mx(
+                out=codes[:].bitcast(FP8X4), scales=plane[:], in_=grouped[:].rearrange("p j t -> p (j t)")
+            )
+            return codes, plane
+
+        def multiply(a, b, codes, plane, c0):
+            for c in range(NT):
+                nc.tensor.matmul_mx(
+                    out=banks[b][:, c, :],
+                    lhsT=w_codes[:, a, 2 * P * c : 2 * P * (c + 1)].bitcast(FP4X4),
+                    lhsT_scale=w_plane[:, a, P * c : P * (c + 1)],
+                    rhs=codes[:, c0 : c0 + BLK].bitcast(FP8X4),
+                    rhs_scale=plane[:, c0 : c0 + BLK],
+                    start=(a == 0 and c == 0),
+                    stop=(a == PASSES - 1 and c == NT - 1),
+                )
+
+        def finish(b):
+            res = keep.tile([P, NT, BLK], F32, name=f"res{b}")
+            cols = slice(b * BLK, (b + 1) * BLK)
+            nc.vector.tensor_tensor(
+                res[:], banks[b][:], slot_w[:, cols].unsqueeze(1).to_broadcast([P, NT, BLK]), MULT
+            )
+            nc.sync.dma_start(out_rows[:, :, cols], res[:])
+
+        pieces = [(0, 0, J, [J]), (1, 0, J // 2, [J // 2]), (1, J // 2, J // 2, [BLK, BLK])]
+        steps = [(i, t) for i in range(len(pieces)) for t in range(PACK)]
+        grouped = [
+            [keep.tile([P, w, PACK], BF16, name=f"g{i}{h}", align_bytes=64) for h, w in enumerate(piece[3])]
+            for i, piece in enumerate(pieces)
+        ]
+        picked = {}
+
+        def first(s):
+            i, t = steps[s]
+            a, j0, width, parts = pieces[i]
+            picked[s, 0] = pick(a, t, list_a, j0, width, f"pa{s}")
+
+        def second(s):
+            i, t = steps[s]
+            a, j0, width, parts = pieces[i]
+            picked[s, 1] = pick(a, t, list_b, j0, width, f"pb{s}")
+
+        def combine(s):
+            i, t = steps[s]
+            a, j0, width, parts = pieces[i]
+            c0 = 0
+            if s == len(steps) - 1:
+                for h, w in enumerate(parts):
+                    m = larger(picked[s, 0], picked[s, 1], c0, w, f"m{s}{h}")
+                    scale(grouped[i][h], m, 0, w, a, t)
+                    c0 = c0 + w
+            else:
+                m = larger(picked[s, 0], picked[s, 1], 0, width, f"m{s}")
+                for h, w in enumerate(parts):
+                    scale(grouped[i][h], m, c0, w, a, t)
+                    c0 = c0 + w
+
+        def product(i):
+            a, j0, width, parts = pieces[i]
+            c0 = j0
+            for h, w in enumerate(parts):
+                codes, plane = quantise(grouped[i][h], w, f"u{i}{h}")
+                for c in range(0, w, BLK):
+                    multiply(a, (c0 + c) // BLK, codes, plane, c)
+                c0 = c0 + w
+
+        first(0)
+        second(0)
+        for s in range(1, len(steps)):
+            first(s)
+            combine(s - 1)
+            second(s)
+            if s % PACK == 1 and s > PACK:
+                product(s // PACK - 1)
+        combine(len(steps) - 1)
+        finish(0)
+        finish(1)
+        product(len(pieces) - 1)
+        finish(2)
+        finish(3)

@@ -42,12 +42,12 @@ def tile_list_head_larger_inputs_kernel(tc, xf, fk, w_words, w_scales, rw, offs,
         slot_w = keep.tile([P, J], F32, name="slot_w")
 
         nc.gpsimd.memset(w_plane[:].rearrange("p a n -> p (a n)").bitcast(I32), 0)
-        nc.sync.dma_start(list_a[:], offs)
         nc.sync.dma_start(x[0][0][:], x_rows[0, 0])
-        nc.sync.dma_start(list_b[:], offs2)
+        nc.sync.dma_start(list_a[:], offs)
         nc.sync.dma_start(x[0][1][:], x_rows[0, 1])
-        nc.sync.dma_start(factor[:], fk.rearrange("(a p t) o -> p a (t o)", a=PASSES, t=PACK))
         nc.sync.dma_start(x[0][2][:], x_rows[0, 2])
+        nc.sync.dma_start(factor[:], fk.rearrange("(a p t) o -> p a (t o)", a=PASSES, t=PACK))
+        nc.sync.dma_start(list_b[:], offs2)
         nc.sync.dma_start(x[0][3][:], x_rows[0, 3])
         for t in range(PACK):
             nc.sync.dma_start(x[1][t][:], x_rows[1, t])
@@ -59,103 +59,112 @@ def tile_list_head_larger_inputs_kernel(tc, xf, fk, w_words, w_scales, rw, offs,
             )
         nc.sync.dma_start(slot_w[:], rw[0].partition_broadcast(P))
 
-        banks = [psum.tile([P, NT, BLK], F32, name=f"bank{b}") for b in range(JB)]
+        split = [1, 1, 2, 2]
+        banks = [
+            [psum.tile([P, NT // split[b], BLK], F32, name=f"bank{b}{h}") for h in range(split[b])] for b in range(JB)
+        ]
         out_rows = out.rearrange("(c p) j -> p c j", p=P)
+        HALF = J // 2
 
-        def pick(a, t, offsets, j0, width, name):
-            picked = keep.tile([P, width], F32, name=name)
-            nc.vector.tensor_copy(picked[:], x[a][t][:].indirect(offsets[:, j0 // 16 : (j0 + width) // 16]))
-            return picked
-
-        def larger(pa, pb, c0, width, name):
-            m = keep.tile([P, width], F32, name=name)
-            nc.vector.tensor_tensor(m[:], pa[:, c0 : c0 + width], pb[:, c0 : c0 + width], MAX)
-            return m
-
-        def scale(grouped, m, c0, width, a, t):
-            nc.scalar.activation(grouped[:, :, t], m[:, c0 : c0 + width], COPY, scale=factor[:, a, t : t + 1])
-
-        def quantise(grouped, width, name):
-            codes = keep.tile([P, width], U32, name=name + "c", align_bytes=64)
-            plane = keep.tile([P, width], U8, name=name + "s", align_bytes=64)
-            nc.vector.quantize_mx(
-                out=codes[:].bitcast(FP8X4), scales=plane[:], in_=grouped[:].rearrange("p j t -> p (j t)")
-            )
-            return codes, plane
-
-        def multiply(a, b, codes, plane, c0):
-            for c in range(NT):
-                nc.tensor.matmul_mx(
-                    out=banks[b][:, c, :],
-                    lhsT=w_codes[:, a, 2 * P * c : 2 * P * (c + 1)].bitcast(FP4X4),
-                    lhsT_scale=w_plane[:, a, P * c : P * (c + 1)],
-                    rhs=codes[:, c0 : c0 + BLK].bitcast(FP8X4),
-                    rhs_scale=plane[:, c0 : c0 + BLK],
-                    start=(a == 0 and c == 0),
-                    stop=(a == PASSES - 1 and c == NT - 1),
-                )
-
-        def finish(b):
-            res = keep.tile([P, NT, BLK], F32, name=f"res{b}")
-            cols = slice(b * BLK, (b + 1) * BLK)
-            nc.vector.tensor_tensor(
-                res[:], banks[b][:], slot_w[:, cols].unsqueeze(1).to_broadcast([P, NT, BLK]), MULT
-            )
-            nc.sync.dma_start(out_rows[:, :, cols], res[:])
-
-        pieces = [(0, 0, J, [J]), (1, 0, J // 2, [J // 2]), (1, J // 2, J // 2, [BLK, BLK])]
-        steps = [(i, t) for i in range(len(pieces)) for t in range(PACK)]
+        spans = [[(0, HALF), (HALF, HALF)], [(0, HALF), (HALF, BLK), (HALF + BLK, BLK)]]
         grouped = [
-            [keep.tile([P, w, PACK], BF16, name=f"g{i}{h}", align_bytes=64) for h, w in enumerate(piece[3])]
-            for i, piece in enumerate(pieces)
+            [keep.tile([P, w, PACK], BF16, name=f"g{a}{h}", align_bytes=64) for h, (j0, w) in enumerate(spans[a])]
+            for a in range(PASSES)
         ]
         picked = {}
+        shared = {
+            "m100": "slot0", "codes01": "slot0",
+            "m110": "slot1", "m12256": "slot1",
+            "m120": "slot2", "p013256": "slot2",
+            "codes10": "slot4", "codes11": "slot4",
+            "plane10": "slot5", "plane12": "slot5",
+            "m130": "slot3", "p113256": "slot3",
+        }
 
-        def first(s):
-            i, t = steps[s]
-            a, j0, width, parts = pieces[i]
-            picked[s, 0] = pick(a, t, list_a, j0, width, f"pa{s}")
+        def pick(which, a, t, j0, width, into=None):
+            offsets = (list_a, list_b)[which]
+            if into is None:
+                name = f"p{which}{a}{t}{j0}"
+                fresh = keep.tile([P, width], F32, name=name, tag=shared.get(name, name), align_bytes=64)
+                into = fresh[:]
+            picked[which, a, t, j0] = into
+            nc.vector.tensor_copy(into, x[a][t][:].indirect(offsets[:, j0 // 16 : (j0 + width) // 16]))
 
-        def second(s):
-            i, t = steps[s]
-            a, j0, width, parts = pieces[i]
-            picked[s, 1] = pick(a, t, list_b, j0, width, f"pb{s}")
+        def scale(m, a, t, j0, width):
+            for h, (s0, w) in enumerate(spans[a]):
+                if j0 <= s0 and s0 + w <= j0 + width:
+                    nc.scalar.activation(
+                        grouped[a][h][:, :, t], m[:, s0 - j0 : s0 - j0 + w], COPY, scale=factor[:, a, t : t + 1]
+                    )
 
-        def combine(s):
-            i, t = steps[s]
-            a, j0, width, parts = pieces[i]
-            c0 = 0
-            if s == len(steps) - 1:
-                for h, w in enumerate(parts):
-                    m = larger(picked[s, 0], picked[s, 1], c0, w, f"m{s}{h}")
-                    scale(grouped[i][h], m, 0, w, a, t)
-                    c0 = c0 + w
-            else:
-                m = larger(picked[s, 0], picked[s, 1], 0, width, f"m{s}")
-                for h, w in enumerate(parts):
-                    scale(grouped[i][h], m, c0, w, a, t)
-                    c0 = c0 + w
+        def combine(a, t, j0, width, c0=0):
+            name = f"m{a}{t}{j0 + c0}"
+            m = keep.tile([P, width], F32, name=name, tag=shared.get(name, name), align_bytes=64)
+            pa, pb = picked[0, a, t, j0], picked[1, a, t, j0]
+            nc.vector.tensor_tensor(m[:], pa[:, c0 : c0 + width], pb[:, c0 : c0 + width], MAX)
+            scale(m, a, t, j0 + c0, width)
 
-        def product(i):
-            a, j0, width, parts = pieces[i]
-            c0 = j0
-            for h, w in enumerate(parts):
-                codes, plane = quantise(grouped[i][h], w, f"u{i}{h}")
-                for c in range(0, w, BLK):
-                    multiply(a, (c0 + c) // BLK, codes, plane, c)
-                c0 = c0 + w
+        def product(a, h):
+            j0, width = spans[a][h]
+            name = f"codes{a}{h}"
+            codes = keep.tile([P, width], U32, name=name, tag=shared.get(name, name), align_bytes=64)
+            name = f"plane{a}{h}"
+            plane = keep.tile([P, width], U8, name=name, tag=shared.get(name, name), align_bytes=64)
+            nc.vector.quantize_mx(
+                out=codes[:].bitcast(FP8X4), scales=plane[:], in_=grouped[a][h][:].rearrange("p j t -> p (j t)")
+            )
+            for c0 in range(0, width, BLK):
+                b = (j0 + c0) // BLK
+                per = NT // split[b]
+                for c in range(NT):
+                    nc.tensor.matmul_mx(
+                        out=banks[b][c // per][:, c % per, :],
+                        lhsT=w_codes[:, a, 2 * P * c : 2 * P * (c + 1)].bitcast(FP4X4),
+                        lhsT_scale=w_plane[:, a, P * c : P * (c + 1)],
+                        rhs=codes[:, c0 : c0 + BLK].bitcast(FP8X4),
+                        rhs_scale=plane[:, c0 : c0 + BLK],
+                        start=(a == 0 and c % per == 0),
+                        stop=(a == PASSES - 1 and c % per == per - 1),
+                    )
 
-        first(0)
-        second(0)
-        for s in range(1, len(steps)):
-            first(s)
-            combine(s - 1)
-            second(s)
-            if s % PACK == 1 and s > PACK:
-                product(s // PACK - 1)
-        combine(len(steps) - 1)
-        finish(0)
-        finish(1)
-        product(len(pieces) - 1)
-        finish(2)
-        finish(3)
+        def finish(b, c0, count, queue):
+            per = NT // split[b]
+            res = keep.tile([P, count, BLK], F32, name=f"res{b}{c0}")
+            cols = slice(b * BLK, (b + 1) * BLK)
+            nc.vector.tensor_tensor(
+                res[:],
+                banks[b][c0 // per][:, c0 % per : c0 % per + count, :],
+                slot_w[:, cols].unsqueeze(1).to_broadcast([P, count, BLK]),
+                MULT,
+            )
+            queue.dma_start(out_rows[:, c0 : c0 + count, cols], res[:])
+
+        whole = [(a, t) for a in range(PASSES) for t in range(PACK)][:6]
+        steps = [(a, t, 0, J) for a, t in whole] + [(1, t, j0, HALF) for j0 in (0, HALF) for t in (2, 3)]
+        pick(0, *steps[0])
+        pick(0, *steps[1])
+        pick(1, *steps[0])
+        pick(1, *steps[1])
+        combine(*steps[0])
+        for s in range(2, len(steps) - 1):
+            pick(0, *steps[s])
+            combine(*steps[s - 1])
+            if s == 6:
+                product(0, 0)
+            pick(1, *steps[s])
+        product(0, 1)
+        combine(*steps[-2])
+        pick(0, *steps[-1])
+        product(1, 0)
+        pick(1, *steps[-1])
+        combine(1, 3, HALF, BLK)
+        combine(1, 3, HALF, BLK, BLK)
+        finish(0, 0, 4, nc.sync)
+        product(1, 1)
+        finish(1, 0, 2, nc.sync)
+        product(1, 2)
+        finish(1, 2, 2, nc.sync)
+        finish(2, 0, 2, nc.sync)
+        finish(2, 2, 2, nc.sync)
+        finish(3, 0, 2, nc.sync)
+        finish(3, 2, 2, nc.scalar)

from contextlib import ExitStack

import concourse.mybir as mybir

K, T, J, N = 1024, 1024, 512, 512
FLOPS = 2 * K * N * J

F32 = mybir.dt.float32
BF16 = mybir.dt.bfloat16
I32 = mybir.dt.int32
U32 = mybir.dt.uint32
U16 = mybir.dt.uint16
U8 = mybir.dt.uint8
FP8X4 = mybir.dt.float8_e4m3fn_x4
FP4X4 = mybir.dt.float4_e2m1fn_x4
MAX = mybir.AluOpType.max
MULT = mybir.AluOpType.mult
COPY = mybir.ActivationFunctionType.Copy

P = 128
PACK = 4
PASSES = K // (P * PACK)
BLK = 128
NT = N // P
JB = J // BLK


def tile_list_head_larger_inputs_kernel(tc, xf, fk, w_words, w_scales, rw, offs, offs2, out):
    nc = tc.nc
    with ExitStack() as ctx:
        lists = ctx.enter_context(tc.tile_pool(name="lists", bufs=1))
        keep = ctx.enter_context(tc.tile_pool(name="keep", bufs=1))
        psum = ctx.enter_context(tc.psum_pool(name="psum", bufs=1))

        list_a = lists.tile([P, J // 16], U16, name="list_a")
        list_b = lists.tile([P, J // 16], U16, name="list_b")
        x_rows = xf.rearrange("(a p t) c -> a t p c", a=PASSES, t=PACK)
        x = [[keep.tile([P, T], F32, name=f"x{a}{t}") for t in range(PACK)] for a in range(PASSES)]
        factor = keep.tile([P, PASSES, PACK], F32, name="factor")
        w_codes = keep.tile([P, PASSES, 2 * N], U8, name="w_codes", align_bytes=64)
        w_plane = keep.tile([P, PASSES, N], U8, name="w_plane", align_bytes=64)
        slot_w = keep.tile([P, J], F32, name="slot_w")

        nc.gpsimd.memset(w_plane[:].rearrange("p a n -> p (a n)").bitcast(I32), 0)
        nc.sync.dma_start(x[0][0][:], x_rows[0, 0])
        nc.sync.dma_start(list_a[:], offs)
        nc.sync.dma_start(x[0][1][:], x_rows[0, 1])
        nc.sync.dma_start(x[0][2][:], x_rows[0, 2])
        nc.sync.dma_start(factor[:], fk.rearrange("(a p t) o -> p a (t o)", a=PASSES, t=PACK))
        nc.sync.dma_start(list_b[:], offs2)
        nc.sync.dma_start(x[0][3][:], x_rows[0, 3])
        for t in range(PACK):
            nc.sync.dma_start(x[1][t][:], x_rows[1, t])
        nc.sync.dma_start(w_codes[:].bitcast(I32), w_words.rearrange("a p n -> p a n").bitcast(I32))
        for q in range(4):
            nc.sync.dma_start(
                w_plane[32 * q : 32 * q + 4].bitcast(I32),
                w_scales[:, 4 * q : 4 * q + 4, :].rearrange("a r n -> r a n").bitcast(I32),
            )
        nc.sync.dma_start(slot_w[:], rw[0].partition_broadcast(P))

        split = [1, 1, 2, 2]
        banks = [
            [psum.tile([P, NT // split[b], BLK], F32, name=f"bank{b}{h}") for h in range(split[b])] for b in range(JB)
        ]
        out_rows = out.rearrange("(c p) j -> p c j", p=P)
        HALF = J // 2

        spans = [[(0, HALF), (HALF, HALF)], [(0, HALF), (HALF, BLK), (HALF + BLK, BLK)]]
        grouped = [
            [keep.tile([P, w, PACK], BF16, name=f"g{a}{h}", align_bytes=64) for h, (j0, w) in enumerate(spans[a])]
            for a in range(PASSES)
        ]
        picked = {}
        shared = {
            "m100": "slot0", "codes01": "slot0",
            "m110": "slot1", "m12256": "slot1",
            "m120": "slot2", "p013256": "slot2",
            "codes10": "slot4", "codes11": "slot4",
            "plane10": "slot5", "plane12": "slot5",
            "m130": "slot3", "p113256": "slot3",
        }

        def pick(which, a, t, j0, width, into=None):
            offsets = (list_a, list_b)[which]
            if into is None:
                name = f"p{which}{a}{t}{j0}"
                fresh = keep.tile([P, width], F32, name=name, tag=shared.get(name, name), align_bytes=64)
                into = fresh[:]
            picked[which, a, t, j0] = into
            nc.vector.tensor_copy(into, x[a][t][:].indirect(offsets[:, j0 // 16 : (j0 + width) // 16]))

        def scale(m, a, t, j0, width):
            for h, (s0, w) in enumerate(spans[a]):
                if j0 <= s0 and s0 + w <= j0 + width:
                    nc.scalar.activation(
                        grouped[a][h][:, :, t], m[:, s0 - j0 : s0 - j0 + w], COPY, scale=factor[:, a, t : t + 1]
                    )

        def combine(a, t, j0, width, c0=0):
            name = f"m{a}{t}{j0 + c0}"
            m = keep.tile([P, width], F32, name=name, tag=shared.get(name, name), align_bytes=64)
            pa, pb = picked[0, a, t, j0], picked[1, a, t, j0]
            nc.vector.tensor_tensor(m[:], pa[:, c0 : c0 + width], pb[:, c0 : c0 + width], MAX)
            scale(m, a, t, j0 + c0, width)

        def product(a, h):
            j0, width = spans[a][h]
            name = f"codes{a}{h}"
            codes = keep.tile([P, width], U32, name=name, tag=shared.get(name, name), align_bytes=64)
            name = f"plane{a}{h}"
            plane = keep.tile([P, width], U8, name=name, tag=shared.get(name, name), align_bytes=64)
            nc.vector.quantize_mx(
                out=codes[:].bitcast(FP8X4), scales=plane[:], in_=grouped[a][h][:].rearrange("p j t -> p (j t)")
            )
            for c0 in range(0, width, BLK):
                b = (j0 + c0) // BLK
                per = NT // split[b]
                for c in range(NT):
                    nc.tensor.matmul_mx(
                        out=banks[b][c // per][:, c % per, :],
                        lhsT=w_codes[:, a, 2 * P * c : 2 * P * (c + 1)].bitcast(FP4X4),
                        lhsT_scale=w_plane[:, a, P * c : P * (c + 1)],
                        rhs=codes[:, c0 : c0 + BLK].bitcast(FP8X4),
                        rhs_scale=plane[:, c0 : c0 + BLK],
                        start=(a == 0 and c % per == 0),
                        stop=(a == PASSES - 1 and c % per == per - 1),
                    )

        def finish(b, c0, count, queue):
            per = NT // split[b]
            res = keep.tile([P, count, BLK], F32, name=f"res{b}{c0}")
            cols = slice(b * BLK, (b + 1) * BLK)
            nc.vector.tensor_tensor(
                res[:],
                banks[b][c0 // per][:, c0 % per : c0 % per + count, :],
                slot_w[:, cols].unsqueeze(1).to_broadcast([P, count, BLK]),
                MULT,
            )
            queue.dma_start(out_rows[:, c0 : c0 + count, cols], res[:])

        whole = [(a, t) for a in range(PASSES) for t in range(PACK)][:6]
        steps = [(a, t, 0, J) for a, t in whole] + [(1, t, j0, HALF) for j0 in (0, HALF) for t in (2, 3)]
        pick(0, *steps[0])
        pick(0, *steps[1])
        pick(1, *steps[0])
        pick(1, *steps[1])
        combine(*steps[0])
        for s in range(2, len(steps) - 1):
            pick(0, *steps[s])
            combine(*steps[s - 1])
            if s == 6:
                product(0, 0)
            pick(1, *steps[s])
        product(0, 1)
        combine(*steps[-2])
        pick(0, *steps[-1])
        product(1, 0)
        pick(1, *steps[-1])
        combine(1, 3, HALF, BLK)
        combine(1, 3, HALF, BLK, BLK)
        finish(0, 0, 4, nc.sync)
        product(1, 1)
        finish(1, 0, 2, nc.sync)
        product(1, 2)
        finish(1, 2, 2, nc.sync)
        finish(2, 0, 2, nc.sync)
        finish(2, 2, 2, nc.sync)
        finish(3, 0, 2, nc.sync)
        finish(3, 2, 2, nc.scalar)
